import numpy as np
import ml_dtypes


def mxq(x, axis, fmt="e4m3"):
    dtype, down = {"e4m3": (ml_dtypes.float8_e4m3fn, 7), "e5m2": (ml_dtypes.float8_e5m2, 14)}[fmt]
    v = np.moveaxis(np.asarray(x, np.float32).astype(ml_dtypes.bfloat16).astype(np.float64), axis, -1)
    blocks = v.reshape(v.shape[:-1] + (-1, 32))
    amax = np.abs(blocks).max(-1, keepdims=True)
    byte = np.maximum(np.where(amax > 0, np.frexp(amax)[1] - 1 + 127, 0) - down, 1)
    scale = np.exp2(byte - 127.0)
    codes = (blocks / scale).astype(np.float32).astype(dtype).astype(np.float64)
    return np.moveaxis((codes * scale).reshape(v.shape), -1, axis)


WIDE = False


def mx_kscale(k):
    if not WIDE:
        return np.ones(k)
    levels = np.array([10, -10, 5, -5, 0])
    if k % 512:
        return np.exp2(np.random.permutation(np.resize(levels, k // 32))).repeat(32)
    a = np.empty((k // 512, 16))
    for p in range(k // 512):
        a[p, :8] = np.random.permutation(np.resize(levels, 8))
        for g in range(8):
            far = levels[np.abs(levels - a[p, g]) >= 10]
            a[p, g + 8] = far[np.random.randint(len(far))]
    return np.exp2(a.ravel()).repeat(32)


def f64(x):
    return np.asarray(x).astype(np.float64)


def striped(idx):
    return np.tile(idx.reshape(-1, 16).T, (8, 1)).astype(np.uint16)


def unstriped(offs):
    return offs[:16].T.reshape(-1).astype(np.int64)


def striped8(idx):
    return np.concatenate([x.reshape(-1, 16).T for x in idx]).astype(np.uint16)


def runs(offs, k):
    lists = np.stack([offs[16 * r : 16 * r + 16].T.reshape(-1) for r in range(8)]).astype(np.int64)
    return lists[np.arange(k) % 512 // 64]


def pack_weight(w):
    k, n = w.shape
    w = f64(np.asarray(w, np.float32).astype(ml_dtypes.bfloat16)).reshape(k // 32, 32, n)
    amax = np.abs(w).max(1)
    byte = np.clip(np.where(amax > 0, np.frexp(amax)[1] - 1 + 127 - 7, 1), 1, 254)
    scaled = (w * np.exp2(127.0 - byte)[:, None, :]).reshape(k, n).astype(np.float32)
    words = np.ascontiguousarray(scaled.reshape(k // 512, 128, 4, n).transpose(0, 1, 3, 2)).astype(ml_dtypes.float8_e4m3fn).view(np.uint8)
    return words, np.ascontiguousarray(byte.astype(np.uint8).reshape(k // 512, 16, n))


def unpack_weight(words, scales):
    g, p, n, _ = words.shape
    vals = np.ascontiguousarray(words).view(ml_dtypes.float8_e4m3fn).astype(np.float64) * np.repeat(np.exp2(scales.astype(np.float64) - 127.0), 8, axis=1)[..., None]
    return vals.transpose(0, 1, 3, 2).reshape(g * 512, n)


K, T, S, V, H, J = 512, 2048, 512, 512, 512, 512


def setup_inputs():
    n = np.random.standard_normal
    s = mx_kscale(K)[:, None]
    u = mx_kscale(S)
    packed_xT = pack_weight(n((K, T)) * s)
    return {
        "x_words": packed_xT[0],
        "x_scales": packed_xT[1],
        "w1": (n((K, H)) / np.sqrt(K) / s).astype(np.float32),
        "w2": (n((K, H)) / np.sqrt(K) / s).astype(np.float32),
        "ga": (np.random.uniform(0.5, 1.5, (H, 1)) * u[:, None]).astype(np.float32),
        "gb": (np.random.uniform(0.5, 1.5, (H, 1)) / u[:, None]).astype(np.float32),
        "tab": np.random.uniform(0.4, 1.4, (S, J)).astype(np.float32),
        "offs": striped(np.random.permutation(T)[:S]),
        "two": striped(np.random.permutation(T)[:V]),
        "n1": striped8(np.stack([np.random.permutation(S) for _ in range(8)])),
        "n2": striped8(np.stack([np.random.permutation(S) for _ in range(8)])),
        "n3": striped8(np.stack([np.random.permutation(S) for _ in range(8)])),
        "n4": striped8(np.stack([np.random.permutation(V) for _ in range(8)])),
        "n5": striped8(np.stack([np.random.permutation(V) for _ in range(8)])),
        "n6": striped8(np.random.randint(0, J, (8, V))),
        "n7": striped8(np.stack([np.random.permutation(V) for _ in range(8)])),
    }


def reference(x_words, x_scales, w1, w2, ga, gb, tab, offs, two, n1, n2, n3, n4, n5, n6, n7):
    xq = unpack_weight(x_words, x_scales)[:, unstriped(offs)]
    a = mxq(f64(w1), 0, "e4m3").T @ xq
    z = f64(ga) * (np.maximum(a, a[np.arange(H)[:, None], runs(n1, H)]) - (np.maximum(a[np.arange(H)[:, None], runs(n2, H)], a[np.arange(H)[:, None], runs(n3, H)])))
    x_two = unpack_weight(x_words, x_scales)[:, unstriped(two)]
    b = mxq(f64(w2), 0, "e4m3").T @ x_two
    st = b + 0.5 * (b[np.arange(H)[:, None], runs(n4, H)])
    z2 = f64(gb) * (st - (st[np.arange(H)[:, None], runs(n5, H)]))
    s = 0.0625 * ((mxq(z, 0, "e4m3").T @ mxq(z2, 0, "e4m3")))
    return s * (f64(tab)[np.arange(S)[:, None], runs(n6, S)]) - (0.5 * (s[np.arange(S)[:, None], runs(n7, S)]))

@@ -1,0 +1,237 @@
+from contextlib import ExitStack
+
+import concourse.mybir as mybir
+
+K, T, S, V, H, J = 512, 2048, 512, 512, 512, 512
+FLOPS = 2 * K * H * S + 2 * K * H * V + 2 * H * S * V
+
+F32 = mybir.dt.float32
+BF16 = mybir.dt.bfloat16
+I32 = mybir.dt.int32
+U32 = mybir.dt.uint32
+U16 = mybir.dt.uint16
+U8 = mybir.dt.uint8
+FP8X4 = mybir.dt.float8_e4m3fn_x4
+ALU = mybir.AluOpType
+COPY = mybir.ActivationFunctionType.Copy
+
+P = 128
+PACK = 4
+N = 512
+HALF = N // 2
+
+
+def tile_picked_kqmixhopkindg_none_p_kernel(tc, x_words, x_scales, w1, w2, ga, gb, tab, offs, two, n1, n2, n3, n4, n5, n6, n7, out):
+    nc = tc.nc
+    with ExitStack() as ctx:
+        keep = ctx.enter_context(tc.tile_pool(name="keep", bufs=1))
+        ring = ctx.enter_context(tc.tile_pool(name="ring", bufs=2))
+        psum = ctx.enter_context(tc.psum_pool(name="psum", bufs=4))
+
+        def load_list(src, name):
+            lst = keep.tile([P, N // 16], U16, name=name)
+            nc.sync.dma_start(lst[:], src)
+            return lst
+
+        def mx_tiles(name, width):
+            codes = keep.tile([P, width], U32, name=name + "_codes", align_bytes=64)
+            scales = keep.tile([P, width], U8, name=name + "_scales", align_bytes=64)
+            return codes, scales
+
+        def quantize(operand, grouped):
+            nc.vector.quantize_mx(out=operand[0][:].bitcast(FP8X4), scales=operand[1][:], in_=grouped[:])
+
+        def product(acc, lhs, t, rhs):
+            cols = slice(t * P, (t + 1) * P)
+            nc.tensor.matmul_mx(out=acc[:], lhsT=lhs[0][:, cols].bitcast(FP8X4), lhsT_scale=lhs[1][:, cols],
+                                rhs=rhs[0][:].bitcast(FP8X4), rhs_scale=rhs[1][:], start=True, stop=True)
+
+        def deal(grouped, planes, m0, m1):
+            nc.scalar.copy(
+                out=grouped[:].rearrange("p (u m j) -> p m j u", u=PACK, j=PACK)[:, m0:m1],
+                in_=planes.rearrange("p j (m u) -> p m j u", u=PACK),
+            )
+
+        xs = keep.tile([P, T], U8, name="xs")
+        nc.vector.memset(xs[:].bitcast(I32), 0)
+        offs_sb = load_list(offs, "offs_sb")
+        two_sb = load_list(two, "two_sb")
+        for q in range(4):
+            nc.scalar.dma_start(xs[32 * q : 32 * q + 4, :].bitcast(I32), x_scales[0, 4 * q : 4 * q + 4, :].bitcast(I32))
+        w1_rows = w1.rearrange("(p j) c -> p j c", j=PACK)
+        w1_raw = []
+        for h in range(2):
+            raw = keep.tile([P, PACK, HALF], F32, name="w1_raw%d" % h)
+            nc.sync.dma_start(raw[:], w1_rows[:, :, h * HALF : (h + 1) * HALF])
+            w1_raw.append(raw)
+        xw = keep.tile([P, T], I32, name="xw")
+        nc.sync.dma_start(xw[:], x_words[0].rearrange("p n t -> p (n t)").bitcast(I32))
+        ga_sb = keep.tile([P, PACK], F32, name="ga_sb")
+        nc.sync.dma_start(ga_sb[:], ga.rearrange("(p t) o -> p (t o)", t=PACK))
+        n1_sb = load_list(n1, "n1_sb")
+        n2_sb = load_list(n2, "n2_sb")
+        n3_sb = load_list(n3, "n3_sb")
+        gb_sb = keep.tile([P, PACK], F32, name="gb_sb")
+        nc.sync.dma_start(gb_sb[:], gb.rearrange("(p t) o -> p (t o)", t=PACK))
+        w2_raw = keep.tile([P, PACK, N], F32, name="w2_raw")
+        nc.sync.dma_start(w2_raw[:], w2.rearrange("(p j) c -> p j c", j=PACK))
+        n4_sb = load_list(n4, "n4_sb")
+        n5_sb = load_list(n5, "n5_sb")
+        tab_raw = keep.tile([P, PACK, N], F32, name="tab_raw")
+        nc.sync.dma_start(tab_raw[:], tab.rearrange("(p t) c -> p t c", t=PACK))
+        n6_sb = load_list(n6, "n6_sb")
+        n7_sb = load_list(n7, "n7_sb")
+
+        win_a = [keep.tile([P, 2 * N], F32, name="win_a%d" % t) for t in range(PACK)]
+        win_b = [keep.tile([P, 2 * N], F32, name="win_b%d" % t) for t in range(PACK)]
+        for win in win_a + win_b:
+            nc.vector.memset(win[:, N:], 0.0)
+
+        sign = keep.tile([P, PACK], F32, name="sign")
+        nc.gpsimd.tensor_scalar(sign[:], ga_sb[:], 0.0, 2.0, ALU.is_ge, ALU.mult)
+        nc.gpsimd.tensor_scalar(sign[:], sign[:], 1.0, -1.0, ALU.mult, ALU.add)
+        ga_abs = keep.tile([P, PACK], F32, name="ga_abs")
+        nc.gpsimd.tensor_tensor(ga_abs[:], ga_sb[:], sign[:], ALU.mult)
+        gb_full = keep.tile([P, PACK], F32, name="gb_full")
+        nc.gpsimd.tensor_tensor(gb_full[:], gb_sb[:], sign[:], ALU.mult)
+        gb_half = keep.tile([P, PACK], F32, name="gb_half")
+        nc.gpsimd.tensor_scalar(gb_half[:], gb_full[:], 0.5, 0.0, ALU.mult, ALU.add)
+
+        xa = mx_tiles("xa", N)
+        xb = mx_tiles("xb", N)
+        nc.vector.tensor_copy(xa[1][:], xs[:].indirect(offs_sb[:]))
+        nc.vector.tensor_copy(xb[1][:], xs[:].indirect(two_sb[:]))
+        w1_grouped = keep.tile([P, PACK * N], BF16, name="w1_grouped", align_bytes=64)
+        for h in range(2):
+            deal(w1_grouped, w1_raw[h][:], h * P // 2, (h + 1) * P // 2)
+        w1q = mx_tiles("w1q", N)
+        quantize(w1q, w1_grouped)
+        nc.vector.tensor_copy(xa[0][:], xw[:].bitcast(U32).indirect(offs_sb[:]))
+        for t in range(PACK):
+            acc = psum.tile([P, N], F32, name="acc_a", tag="bank_a")
+            product(acc, w1q, t, xa)
+            nc.scalar.activation(win_a[t][:, :N], acc[:], COPY, scale=ga_abs[:, t : t + 1])
+        nc.vector.tensor_copy(xb[0][:], xw[:].bitcast(U32).indirect(two_sb[:]))
+
+        w2_grouped = keep.tile([P, PACK * N], BF16, name="w2_grouped", align_bytes=64)
+        deal(w2_grouped, w2_raw[:], 0, P)
+        w2q = mx_tiles("w2q", N)
+
+        z_planes = keep.tile([P, PACK, N], F32, name="z_planes")
+        first = {}
+        top = {}
+        gaps = {}
+
+        def fetch_first(t):
+            first[t] = ring.tile([P, N], F32, name="first")
+            nc.vector.tensor_copy(first[t][:], win_a[t][:].indirect(n1_sb[:]))
+
+        def larger_first(t):
+            top[t] = ring.tile([P, N], F32, name="top")
+            nc.vector.tensor_tensor(top[t][:], win_a[t][:, :N], first[t][:], ALU.max)
+
+        def gap(t, i, lst):
+            gaps[t, i] = ring.tile([P, N], F32, name="gap%d" % i)
+            nc.vector.tensor_tensor(gaps[t, i][:], win_a[t][:].indirect(lst[:]), top[t][:], ALU.subtract)
+
+        def larger_gap(t):
+            nc.vector.tensor_tensor(z_planes[:, t, :], gaps[t, 0][:], gaps[t, 1][:], ALU.max)
+
+        b_full = [keep.tile([P, N], F32, name="b_full%d" % t) for t in range(PACK)]
+
+        def make_b():
+            quantize(w2q, w2_grouped)
+            for t in range(PACK):
+                acc = psum.tile([P, N], F32, name="acc_b", tag="bank_b")
+                product(acc, w2q, t, xb)
+                nc.scalar.activation(win_b[t][:, :N], acc[:], COPY, scale=gb_half[:, t : t + 1])
+                nc.scalar.activation(b_full[t][:], acc[:], COPY, scale=gb_full[:, t : t + 1])
+
+        fetch_first(0)
+        fetch_first(1)
+        larger_first(0)
+        for t in range(PACK):
+            gap(t, 0, n2_sb)
+            if t + 1 < PACK:
+                larger_first(t + 1)
+            gap(t, 1, n3_sb)
+            if t + 2 < PACK:
+                fetch_first(t + 2)
+            if t == 1:
+                make_b()
+            if t > 0:
+                larger_gap(t - 1)
+
+        st = [keep.tile([P, N], F32, name="st%d" % t) for t in range(PACK)]
+        win_st = [keep.tile([P, N], F32, name="win_st%d" % t) for t in range(PACK)]
+        z_grouped = keep.tile([P, PACK * N], BF16, name="z_grouped", align_bytes=64)
+        zq = mx_tiles("zq", N)
+        for t in range(PACK):
+            nc.vector.tensor_tensor(st[t][:], win_b[t][:].indirect(n4_sb[:]), b_full[t][:], ALU.add)
+            nc.scalar.copy(win_st[t][:], st[t][:])
+            if t == 0:
+                larger_gap(PACK - 1)
+                deal(z_grouped, z_planes[:], 0, P)
+        win_tab = [keep.tile([P, N], F32, name="win_tab%d" % t) for t in range(PACK)]
+        for t in range(PACK):
+            nc.scalar.activation(win_tab[t][:], tab_raw[:, t, :], COPY, scale=-2.0)
+        quantize(zq, z_grouped)
+
+        z2_planes = [keep.tile([P, PACK, HALF], F32, name="z2_planes%d" % h) for h in range(2)]
+        z2_grouped = [keep.tile([P, PACK * HALF], BF16, name="z2_grouped%d" % h, align_bytes=64) for h in range(2)]
+        z2q = [mx_tiles("z2q%d" % h, HALF) for h in range(2)]
+        scaled = [keep.tile([P, N], F32, name="scaled%d" % t) for t in range(PACK)]
+
+        def entries(lst, h):
+            return lst[:, h * HALF // 16 : (h + 1) * HALF // 16]
+
+        def hop(h, t):
+            nc.vector.tensor_tensor(z2_planes[h][:, t, :], win_st[t][:].indirect(entries(n5_sb, h)),
+                                    st[t][:, h * HALF : (h + 1) * HALF], ALU.subtract)
+
+        def group_z2(h):
+            nc.scalar.copy(
+                out=z2_grouped[h][:].rearrange("p (c i t) -> p c t i", i=4, t=PACK),
+                in_=z2_planes[h][:].rearrange("p t (c i) -> p c t i", i=4),
+            )
+
+        def make_s(h, t):
+            acc = psum.tile([P, HALF], F32, name="acc_s", tag=("bank_a", "bank_b")[h])
+            product(acc, zq, t, z2q[h])
+            nc.scalar.activation(win_a[t][:, h * HALF : (h + 1) * HALF], acc[:], COPY, scale=-0.03125)
+
+        def weigh(h, t):
+            cols = slice(h * HALF, (h + 1) * HALF)
+            nc.vector.tensor_tensor(scaled[t][:, cols], win_tab[t][:].indirect(entries(n6_sb, h)), win_a[t][:, cols], ALU.mult)
+
+        out_rows = out.rearrange("(p t) v -> p t v", t=PACK)
+
+        def finish(t):
+            res = keep.tile([P, N], F32, name="res%d" % t)
+            nc.vector.tensor_tensor(res[:], win_a[t][:].indirect(n7_sb[:]), scaled[t][:], ALU.add)
+            nc.sync.dma_start(out_rows[:, t, :], res[:])
+
+        for t in range(PACK):
+            hop(0, t)
+        group_z2(0)
+        for t in range(PACK - 1):
+            hop(1, t)
+        quantize(z2q[0], z2_grouped[0])
+        hop(1, PACK - 1)
+        make_s(0, 0)
+        make_s(0, 1)
+        group_z2(1)
+        make_s(0, 2)
+        make_s(0, 3)
+        weigh(0, 0)
+        weigh(0, 1)
+        quantize(z2q[1], z2_grouped[1])
+        for t in range(PACK):
+            make_s(1, t)
+        weigh(0, 2)
+        weigh(0, 3)
+        weigh(1, 0)
+        for t in range(PACK):
+            if t + 1 < PACK:
+                weigh(1, t + 1)
+            finish(t)

@@ -1,6 +1,7 @@
 from contextlib import ExitStack
 
 import concourse.mybir as mybir
+from concourse.masks import make_identity
 
 K, T, S, V, H, J = 512, 2048, 512, 512, 512, 512
 FLOPS = 2 * K * H * S + 2 * K * H * V + 2 * H * S * V
@@ -14,18 +15,22 @@ U8 = mybir.dt.uint8
 FP8X4 = mybir.dt.float8_e4m3fn_x4
 ALU = mybir.AluOpType
 COPY = mybir.ActivationFunctionType.Copy
+RELU = mybir.ActivationFunctionType.Relu
+ABS = mybir.ActivationFunctionType.Abs
+SIGN = mybir.ActivationFunctionType.Sign
 
 P = 128
 PACK = 4
 N = 512
 HALF = N // 2
+ON_VECTOR = (0, 2, 3)
 
 
 def tile_picked_kqmixhopkindg_none_p_kernel(tc, x_words, x_scales, w1, w2, ga, gb, tab, offs, two, n1, n2, n3, n4, n5, n6, n7, out):
     nc = tc.nc
     with ExitStack() as ctx:
         keep = ctx.enter_context(tc.tile_pool(name="keep", bufs=1))
-        ring = ctx.enter_context(tc.tile_pool(name="ring", bufs=2))
+        ring = ctx.enter_context(tc.tile_pool(name="ring", bufs=4))
         psum = ctx.enter_context(tc.psum_pool(name="psum", bufs=4))
 
         def load_list(src, name):
@@ -39,7 +44,7 @@ def tile_picked_kqmixhopkindg_none_p_kernel(tc, x_words, x_scales, w1, w2, ga, g
             return codes, scales
 
         def quantize(operand, grouped):
-            nc.vector.quantize_mx(out=operand[0][:].bitcast(FP8X4), scales=operand[1][:], in_=grouped[:])
+            nc.vector.quantize_mx(out=operand[0][:].bitcast(FP8X4), scales=operand[1][:], in_=grouped)
 
         def product(acc, lhs, t, rhs):
             cols = slice(t * P, (t + 1) * P)
@@ -53,185 +58,264 @@ def tile_picked_kqmixhopkindg_none_p_kernel(tc, x_words, x_scales, w1, w2, ga, g
             )
 
         xs = keep.tile([P, T], U8, name="xs")
-        nc.vector.memset(xs[:].bitcast(I32), 0)
+        nc.gpsimd.memset(xs[:].bitcast(I32), 0)
         offs_sb = load_list(offs, "offs_sb")
-        two_sb = load_list(two, "two_sb")
-        for q in range(4):
-            nc.scalar.dma_start(xs[32 * q : 32 * q + 4, :].bitcast(I32), x_scales[0, 4 * q : 4 * q + 4, :].bitcast(I32))
         w1_rows = w1.rearrange("(p j) c -> p j c", j=PACK)
-        w1_raw = []
-        for h in range(2):
-            raw = keep.tile([P, PACK, HALF], F32, name="w1_raw%d" % h)
-            nc.sync.dma_start(raw[:], w1_rows[:, :, h * HALF : (h + 1) * HALF])
-            w1_raw.append(raw)
+        w1_raw = [keep.tile([P, PACK, HALF], F32, name="w1_raw%d" % h, tag="w_raw%d" % h, align_bytes=64) for h in range(2)]
+        nc.sync.dma_start(w1_raw[0][:], w1_rows[:, :, :HALF])
+        for q in range(4):
+            nc.sync.dma_start(xs[32 * q : 32 * q + 4, :].bitcast(I32), x_scales[0, 4 * q : 4 * q + 4, :].bitcast(I32))
+        two_sb = load_list(two, "two_sb")
+        nc.sync.dma_start(w1_raw[1][:], w1_rows[:, :, HALF:])
         xw = keep.tile([P, T], I32, name="xw")
         nc.sync.dma_start(xw[:], x_words[0].rearrange("p n t -> p (n t)").bitcast(I32))
         ga_sb = keep.tile([P, PACK], F32, name="ga_sb")
         nc.sync.dma_start(ga_sb[:], ga.rearrange("(p t) o -> p (t o)", t=PACK))
-        n1_sb = load_list(n1, "n1_sb")
         n2_sb = load_list(n2, "n2_sb")
         n3_sb = load_list(n3, "n3_sb")
+        n1_sb = load_list(n1, "n1_sb")
         gb_sb = keep.tile([P, PACK], F32, name="gb_sb")
         nc.sync.dma_start(gb_sb[:], gb.rearrange("(p t) o -> p (t o)", t=PACK))
-        w2_raw = keep.tile([P, PACK, N], F32, name="w2_raw")
+        w2_raw = keep.tile([P, PACK, N], F32, name="w2_raw", tag="w2_raw", align_bytes=64)
         nc.sync.dma_start(w2_raw[:], w2.rearrange("(p j) c -> p j c", j=PACK))
         n4_sb = load_list(n4, "n4_sb")
         n5_sb = load_list(n5, "n5_sb")
-        tab_raw = keep.tile([P, PACK, N], F32, name="tab_raw")
-        nc.sync.dma_start(tab_raw[:], tab.rearrange("(p t) c -> p t c", t=PACK))
         n6_sb = load_list(n6, "n6_sb")
         n7_sb = load_list(n7, "n7_sb")
 
         win_a = [keep.tile([P, 2 * N], F32, name="win_a%d" % t) for t in range(PACK)]
         win_b = [keep.tile([P, 2 * N], F32, name="win_b%d" % t) for t in range(PACK)]
-        for win in win_a + win_b:
-            nc.vector.memset(win[:, N:], 0.0)
+        for win in win_a:
+            nc.gpsimd.memset(win[:, N:], 0.0)
+        ident = keep.tile([P, P], F32, name="ident")
+        make_identity(nc, ident[:])
 
-        sign = keep.tile([P, PACK], F32, name="sign")
-        nc.gpsimd.tensor_scalar(sign[:], ga_sb[:], 0.0, 2.0, ALU.is_ge, ALU.mult)
-        nc.gpsimd.tensor_scalar(sign[:], sign[:], 1.0, -1.0, ALU.mult, ALU.add)
         ga_abs = keep.tile([P, PACK], F32, name="ga_abs")
-        nc.gpsimd.tensor_tensor(ga_abs[:], ga_sb[:], sign[:], ALU.mult)
+        nc.scalar.activation(ga_abs[:], ga_sb[:], ABS)
+        sign3 = keep.tile([P, PACK], F32, name="sign3")
+        nc.scalar.activation(sign3[:], ga_sb[:], SIGN)
+        sign = keep.tile([P, PACK], F32, name="sign")
+        nc.scalar.activation(sign[:], sign3[:], SIGN, bias=0.5)
         gb_full = keep.tile([P, PACK], F32, name="gb_full")
-        nc.gpsimd.tensor_tensor(gb_full[:], gb_sb[:], sign[:], ALU.mult)
+        for t in range(PACK):
+            nc.scalar.activation(gb_full[:, t : t + 1], gb_sb[:, t : t + 1], COPY, scale=sign[:, t : t + 1])
         gb_half = keep.tile([P, PACK], F32, name="gb_half")
-        nc.gpsimd.tensor_scalar(gb_half[:], gb_full[:], 0.5, 0.0, ALU.mult, ALU.add)
+        nc.scalar.activation(gb_half[:], gb_full[:], COPY, scale=0.5)
 
-        xa = mx_tiles("xa", N)
+        xa_scales = keep.tile([P, N], U8, name="xa_scales", align_bytes=64)
+        xa_codes = [keep.tile([P, HALF], U32, name="xa_codes%d" % h, align_bytes=64) for h in range(2)]
         xb = mx_tiles("xb", N)
-        nc.vector.tensor_copy(xa[1][:], xs[:].indirect(offs_sb[:]))
+        nc.vector.tensor_copy(xa_scales[:], xs[:].indirect(offs_sb[:]))
         nc.vector.tensor_copy(xb[1][:], xs[:].indirect(two_sb[:]))
         w1_grouped = keep.tile([P, PACK * N], BF16, name="w1_grouped", align_bytes=64)
         for h in range(2):
             deal(w1_grouped, w1_raw[h][:], h * P // 2, (h + 1) * P // 2)
         w1q = mx_tiles("w1q", N)
-        quantize(w1q, w1_grouped)
-        nc.vector.tensor_copy(xa[0][:], xw[:].bitcast(U32).indirect(offs_sb[:]))
+        quantize(w1q, w1_grouped[:])
+        xa = [(xa_codes[h], xa_scales[:, h * HALF : (h + 1) * HALF]) for h in range(2)]
+        for h in range(2):
+            nc.vector.tensor_copy(xa_codes[h][:], xw[:].bitcast(U32).indirect(offs_sb[:, h * HALF // 16 : (h + 1) * HALF // 16]))
+        last_copy = keep.tile([P, N], F32, name="last_copy", tag="st")
+        a_copy = [win_b[t][:, N:] for t in range(PACK - 1)] + [last_copy[:]]
+        w2q = mx_tiles("w2q", N)
         for t in range(PACK):
-            acc = psum.tile([P, N], F32, name="acc_a", tag="bank_a")
-            product(acc, w1q, t, xa)
+            acc = psum.tile([P, N], F32, name="acc_a", tag="bank_mm")
+            for h in range(2):
+                product(acc[:, h * HALF : (h + 1) * HALF], w1q, t, xa[h])
             nc.scalar.activation(win_a[t][:, :N], acc[:], COPY, scale=ga_abs[:, t : t + 1])
+            if t < 2:
+                nc.scalar.activation(a_copy[t], acc[:], COPY, scale=ga_abs[:, t : t + 1])
+            else:
+                nc.sync.dma_start(a_copy[t], win_a[t][:, :N])
+        w2_grouped = keep.tile([P, PACK * N], BF16, name="w2_grouped", tag="w2_stage", align_bytes=64)
+        deal(w2_grouped, w2_raw[:], 0, P)
         nc.vector.tensor_copy(xb[0][:], xw[:].bitcast(U32).indirect(two_sb[:]))
 
-        w2_grouped = keep.tile([P, PACK * N], BF16, name="w2_grouped", align_bytes=64)
-        deal(w2_grouped, w2_raw[:], 0, P)
-        w2q = mx_tiles("w2q", N)
+        sums = [psum.tile([P, PACK, P], F32, name="sums%d" % jb, tag="bank_sum") for jb in range(PACK)]
+        late = keep.tile([P, 6 * N], F32, name="late", tag="w2_raw", align_bytes=64)
+        early = keep.tile([P, 3 * N], F32, name="early", tag="early", align_bytes=64)
+        second = [win_b[PACK - 1][:, N:], early[:, :N], late[:, :N], late[:, N : 2 * N]]
+        rise1 = [early[:, N : 2 * N], early[:, 2 * N :], late[:, 2 * N : 3 * N], late[:, 3 * N : 4 * N]]
+        up1_tiles = [ring.tile([P, N], F32, name="up1") for t in range(PACK)]
+        up3_tiles = [ring.tile([P, N], F32, name="up3") for t in range(PACK)]
+        up1 = [late[:, 4 * N : 5 * N] if t == 1 else up1_tiles[t][:] for t in range(PACK)]
+        up3 = [late[:, 5 * N :] if t == 1 else up3_tiles[t][:] for t in range(PACK)]
+        rise3 = [ring.tile([P, N], F32, name="rise3") for t in range(PACK)]
+        down3 = [ring.tile([P, N], F32, name="down3") for t in range(PACK)]
 
-        z_planes = keep.tile([P, PACK, N], F32, name="z_planes")
-        first = {}
-        top = {}
-        gaps = {}
+        def fetch2(t):
+            nc.vector.tensor_scalar(second[t], win_a[t][:].indirect(n2_sb[:]), -1.0, 0.0, ALU.mult, ALU.add)
 
-        def fetch_first(t):
-            first[t] = ring.tile([P, N], F32, name="first")
-            nc.vector.tensor_copy(first[t][:], win_a[t][:].indirect(n1_sb[:]))
+        def fetch1(t):
+            nc.vector.tensor_tensor(rise1[t], win_a[t][:].indirect(n1_sb[:]), a_copy[t], ALU.subtract)
+            nc.scalar.activation(up1[t], rise1[t], RELU)
 
-        def larger_first(t):
-            top[t] = ring.tile([P, N], F32, name="top")
-            nc.vector.tensor_tensor(top[t][:], win_a[t][:, :N], first[t][:], ALU.max)
+        def fetch3(t):
+            nc.vector.tensor_tensor(rise3[t][:], win_a[t][:].indirect(n3_sb[:]), second[t], ALU.add)
 
-        def gap(t, i, lst):
-            gaps[t, i] = ring.tile([P, N], F32, name="gap%d" % i)
-            nc.vector.tensor_tensor(gaps[t, i][:], win_a[t][:].indirect(lst[:]), top[t][:], ALU.subtract)
+        def clip3(t):
+            if t in ON_VECTOR:
+                nc.vector.tensor_scalar(down3[t][:], rise3[t][:], 0.0, -1.0, ALU.max, ALU.mult)
+            else:
+                nc.scalar.activation(up3[t], rise3[t][:], RELU)
+                nc.scalar.activation(down3[t][:], up3[t], COPY, scale=-1.0)
 
-        def larger_gap(t):
-            nc.vector.tensor_tensor(z_planes[:, t, :], gaps[t, 0][:], gaps[t, 1][:], ALU.max)
+        def add_up(t):
+            addends = [win_a[t][:, :N], second[t], down3[t][:], up1[t]]
+            for i, addend in enumerate(addends):
+                for jb in range(PACK):
+                    nc.tensor.matmul(sums[jb][:, t, :], addend[:, jb * P : (jb + 1) * P], ident[:],
+                                     start=(i == 0), stop=(i == len(addends) - 1), is_transpose=True)
 
-        b_full = [keep.tile([P, N], F32, name="b_full%d" % t) for t in range(PACK)]
+        b_full = [keep.tile([P, N], F32, name="b_full%d" % t, tag="b_full%d" % t, align_bytes=64) for t in range(PACK)]
 
-        def make_b():
-            quantize(w2q, w2_grouped)
-            for t in range(PACK):
-                acc = psum.tile([P, N], F32, name="acc_b", tag="bank_b")
-                product(acc, w2q, t, xb)
-                nc.scalar.activation(win_b[t][:, :N], acc[:], COPY, scale=gb_half[:, t : t + 1])
-                nc.scalar.activation(b_full[t][:], acc[:], COPY, scale=gb_full[:, t : t + 1])
+        def make_b(t):
+            acc = b_acc[t]
+            nc.scalar.activation(win_b[t][:, :N], acc[:], COPY, scale=gb_half[:, t : t + 1])
+            nc.scalar.activation(b_full[t][:], acc[:], COPY, scale=gb_full[:, t : t + 1])
 
-        fetch_first(0)
-        fetch_first(1)
-        larger_first(0)
+        for t in range(2):
+            fetch2(t)
+            fetch1(t)
+            fetch3(t)
+            clip3(t)
+        add_up(0)
+        quantize(w2q, w2_grouped[:])
+        b_acc = [psum.tile([P, N], F32, name="acc_b", tag="bank_mm") for t in range(PACK)]
         for t in range(PACK):
-            gap(t, 0, n2_sb)
-            if t + 1 < PACK:
-                larger_first(t + 1)
-            gap(t, 1, n3_sb)
-            if t + 2 < PACK:
-                fetch_first(t + 2)
-            if t == 1:
-                make_b()
-            if t > 0:
-                larger_gap(t - 1)
+            product(b_acc[t], w2q, t, xb)
+        add_up(1)
+        make_b(0)
+        make_b(1)
+        make_b(2)
+        fetch2(2)
+        fetch1(2)
+        fetch3(2)
+        fetch2(3)
+        clip3(2)
+        make_b(3)
+        add_up(2)
+        fetch3(3)
+        fetch1(3)
+        clip3(3)
+        add_up(3)
 
-        st = [keep.tile([P, N], F32, name="st%d" % t) for t in range(PACK)]
-        win_st = [keep.tile([P, N], F32, name="win_st%d" % t) for t in range(PACK)]
-        z_grouped = keep.tile([P, PACK * N], BF16, name="z_grouped", align_bytes=64)
-        zq = mx_tiles("zq", N)
+        tab_tags = ["w_raw0", "w_raw1", "w2_stage", "early"]
+        win_tab = [keep.tile([P, N], F32, name="win_tab%d" % t, tag=tab_tags[t], align_bytes=64) for t in range(PACK)]
         for t in range(PACK):
-            nc.vector.tensor_tensor(st[t][:], win_b[t][:].indirect(n4_sb[:]), b_full[t][:], ALU.add)
-            nc.scalar.copy(win_st[t][:], st[t][:])
-            if t == 0:
-                larger_gap(PACK - 1)
-                deal(z_grouped, z_planes[:], 0, P)
-        win_tab = [keep.tile([P, N], F32, name="win_tab%d" % t) for t in range(PACK)]
-        for t in range(PACK):
-            nc.scalar.activation(win_tab[t][:], tab_raw[:, t, :], COPY, scale=-2.0)
-        quantize(zq, z_grouped)
+            nc.sync.dma_start(win_tab[t][:], tab.rearrange("(p t) c -> p t c", t=PACK)[:, t, :])
 
-        z2_planes = [keep.tile([P, PACK, HALF], F32, name="z2_planes%d" % h) for h in range(2)]
-        z2_grouped = [keep.tile([P, PACK * HALF], BF16, name="z2_grouped%d" % h, align_bytes=64) for h in range(2)]
-        z2q = [mx_tiles("z2q%d" % h, HALF) for h in range(2)]
-        scaled = [keep.tile([P, N], F32, name="scaled%d" % t) for t in range(PACK)]
+        st_all = keep.tile([P, PACK * N], F32, name="st_all", tag="st")
+        st = [st_all[:, t * N : (t + 1) * N] for t in range(PACK)]
+        win_st = {}
 
         def entries(lst, h):
             return lst[:, h * HALF // 16 : (h + 1) * HALF // 16]
 
+        def make_st(t):
+            nc.vector.tensor_tensor(st[t], win_b[t][:].indirect(n4_sb[:]), b_full[t][:], ALU.add)
+
+        def copy_st(t):
+            win_st[t] = keep.tile([P, N], F32, name="win_st%d" % t, tag="turn%d" % t if t > 0 else "win_st0")
+            if t < 1:
+                nc.sync.dma_start(win_st[t][:], st[t])
+            else:
+                nc.scalar.copy(win_st[t][:], st[t])
+
+        for t in range(PACK):
+            make_st(t)
+        stage = keep.tile([P, 4 * N], F32, name="stage", tag="b_full2", align_bytes=64)
+        z_stage = stage[:, : 2 * N]
+        z_words = z_stage.rearrange("p (u b m e) -> p b m e u", u=PACK, b=PACK, e=2)
+        back = [psum.tile([P, 2, 2, P], F32, name="back", tag="bank_mm") for pair in range(2)]
+
+        def turn_back(jb):
+            pair, b = divmod(jb, 2)
+            turned = keep.tile([P, N], BF16, name="turned%d" % jb, tag="turn%d" % jb)
+            nc.scalar.copy(out=turned[:].rearrange("j (e p i) -> j e p i", e=2, i=2),
+                           in_=sums[jb][:].rearrange("j (e i) p -> j e p i", i=2))
+            for e in range(2):
+                nc.tensor.transpose(back[pair][:, b, e, :], turned[:].bitcast(F32)[:, e * P : (e + 1) * P], ident[:])
+
+        def deal_z(pair):
+            nc.scalar.copy(out=z_words[:, 2 * pair : 2 * pair + 2], in_=back[pair][:].rearrange("p b e (m u) -> p b m e u", u=PACK))
+
+        for t in range(PACK):
+            turn_back(t)
+            copy_st(t)
+            if t % 2 == 1:
+                deal_z(t // 2)
+        zq = mx_tiles("zq", N)
+
+        z2_planes = [stage[:, 2 * N :], stage[:, N : 3 * N]]
+        z2_grouped = [keep.tile([P, PACK * HALF], BF16, name="z2_grouped%d" % h, align_bytes=64) for h in range(2)]
+        z2q = [mx_tiles("z2q%d" % h, HALF) for h in range(2)]
+        s_rows = [keep.tile([P, N], F32, name="s_rows%d" % t) for t in range(PACK)]
+        scaled = {}
+        s_acc = {}
+
         def hop(h, t):
-            nc.vector.tensor_tensor(z2_planes[h][:, t, :], win_st[t][:].indirect(entries(n5_sb, h)),
+            nc.vector.tensor_tensor(z2_planes[h][:, t * HALF : (t + 1) * HALF], win_st[t][:].indirect(entries(n5_sb, h)),
                                     st[t][:, h * HALF : (h + 1) * HALF], ALU.subtract)
 
         def group_z2(h):
             nc.scalar.copy(
                 out=z2_grouped[h][:].rearrange("p (c i t) -> p c t i", i=4, t=PACK),
-                in_=z2_planes[h][:].rearrange("p t (c i) -> p c t i", i=4),
+                in_=z2_planes[h].rearrange("p (t c i) -> p c t i", i=4, t=PACK),
             )
 
         def make_s(h, t):
-            acc = psum.tile([P, HALF], F32, name="acc_s", tag=("bank_a", "bank_b")[h])
-            product(acc, zq, t, z2q[h])
-            nc.scalar.activation(win_a[t][:, h * HALF : (h + 1) * HALF], acc[:], COPY, scale=-0.03125)
+            s_acc[h, t] = psum.tile([P, HALF], F32, name="acc_s", tag=("bank_mm", "bank_sum")[h])
+            product(s_acc[h, t], zq, t, z2q[h])
+            nc.scalar.activation(s_rows[t][:, h * HALF : (h + 1) * HALF], s_acc[h, t][:], COPY, scale=-0.0625)
+
+        def halve_s(h, t):
+            nc.scalar.activation(win_a[t][:, h * HALF : (h + 1) * HALF], s_acc[h, t][:], COPY, scale=0.03125)
 
         def weigh(h, t):
             cols = slice(h * HALF, (h + 1) * HALF)
-            nc.vector.tensor_tensor(scaled[t][:, cols], win_tab[t][:].indirect(entries(n6_sb, h)), win_a[t][:, cols], ALU.mult)
+            nc.vector.tensor_tensor(scaled[t][:, cols], win_tab[t][:].indirect(entries(n6_sb, h)), s_rows[t][:, cols], ALU.mult)
 
         out_rows = out.rearrange("(p t) v -> p t v", t=PACK)
 
-        def finish(t):
-            res = keep.tile([P, N], F32, name="res%d" % t)
-            nc.vector.tensor_tensor(res[:], win_a[t][:].indirect(n7_sb[:]), scaled[t][:], ALU.add)
-            nc.sync.dma_start(out_rows[:, t, :], res[:])
+        def finish(t, pieces):
+            width = N // pieces
+            for i in range(pieces):
+                cols = slice(i * width, (i + 1) * width)
+                res = keep.tile([P, width], F32, name="res%d_%d" % (t, i))
+                nc.vector.tensor_tensor(res[:], win_a[t][:].indirect(n7_sb[:, i * width // 16 : (i + 1) * width // 16]), scaled[t][:, cols], ALU.add)
+                nc.sync.dma_start(out_rows[:, t, cols], res[:])
 
         for t in range(PACK):
             hop(0, t)
+        quantize(zq, z_stage.bitcast(BF16))
         group_z2(0)
-        for t in range(PACK - 1):
-            hop(1, t)
-        quantize(z2q[0], z2_grouped[0])
-        hop(1, PACK - 1)
+        hop(1, 0)
+        hop(1, 1)
+        quantize(z2q[0], z2_grouped[0][:])
+        hop(1, 2)
+        hop(1, 3)
         make_s(0, 0)
         make_s(0, 1)
         group_z2(1)
         make_s(0, 2)
         make_s(0, 3)
+        front = keep.tile([P, 2 * N], F32, name="front")
+        scaled[0], scaled[1] = front[:, :N], front[:, N:]
+        scaled[2], scaled[3] = stage[:, N : 2 * N], stage[:, 2 * N : 3 * N]
         weigh(0, 0)
         weigh(0, 1)
-        quantize(z2q[1], z2_grouped[1])
-        for t in range(PACK):
-            make_s(1, t)
+        quantize(z2q[1], z2_grouped[1][:])
         weigh(0, 2)
         weigh(0, 3)
+        make_s(1, 0)
+        for t in range(PACK):
+            if t + 1 < PACK:
+                make_s(1, t + 1)
+            halve_s(0, t)
+            halve_s(1, t)
         weigh(1, 0)
         for t in range(PACK):
             if t + 1 < PACK:
                 weigh(1, t + 1)
-            finish(t)
+            finish(t, 2 if t == PACK - 1 else 1)

@@ -3,7 +3,7 @@ from contextlib import ExitStack
 import concourse.mybir as mybir
 from concourse.masks import make_identity
 
-K, T, S, V, H, J = 512, 2048, 512, 512, 512, 512
+K, S, V, H = 512, 512, 512, 512
 FLOPS = 2 * K * H * S + 2 * K * H * V + 2 * H * S * V
 
 F32 = mybir.dt.float32
@@ -21,22 +21,28 @@ SIGN = mybir.ActivationFunctionType.Sign
 
 P = 128
 PACK = 4
+TOKENS = 2048
 N = 512
 HALF = N // 2
-ON_VECTOR = (0, 2, 3)
+LANES = 16
+CLIP_ON_SCALAR = 1
+A_BY_SCALAR = 2
+ST_BY_DMA = 2
 
 
 def tile_picked_kqmixhopkindg_none_p_kernel(tc, x_words, x_scales, w1, w2, ga, gb, tab, offs, two, n1, n2, n3, n4, n5, n6, n7, out):
     nc = tc.nc
     with ExitStack() as ctx:
         keep = ctx.enter_context(tc.tile_pool(name="keep", bufs=1))
-        ring = ctx.enter_context(tc.tile_pool(name="ring", bufs=4))
-        psum = ctx.enter_context(tc.psum_pool(name="psum", bufs=4))
+        psum = ctx.enter_context(tc.psum_pool(name="psum", bufs=PACK))
 
         def load_list(src, name):
-            lst = keep.tile([P, N // 16], U16, name=name)
+            lst = keep.tile([P, N // LANES], U16, name=name)
             nc.sync.dma_start(lst[:], src)
             return lst
+
+        def entries(lst, h):
+            return lst[:, h * HALF // LANES : (h + 1) * HALF // LANES]
 
         def mx_tiles(name, width):
             codes = keep.tile([P, width], U32, name=name + "_codes", align_bytes=64)
@@ -51,23 +57,23 @@ def tile_picked_kqmixhopkindg_none_p_kernel(tc, x_words, x_scales, w1, w2, ga, g
             nc.tensor.matmul_mx(out=acc[:], lhsT=lhs[0][:, cols].bitcast(FP8X4), lhsT_scale=lhs[1][:, cols],
                                 rhs=rhs[0][:].bitcast(FP8X4), rhs_scale=rhs[1][:], start=True, stop=True)
 
-        def deal(grouped, planes, m0, m1):
+        def deal_weights(grouped, raw, m0, m1):
             nc.scalar.copy(
                 out=grouped[:].rearrange("p (u m j) -> p m j u", u=PACK, j=PACK)[:, m0:m1],
-                in_=planes.rearrange("p j (m u) -> p m j u", u=PACK),
+                in_=raw.rearrange("p j (m u) -> p m j u", u=PACK),
             )
 
-        xs = keep.tile([P, T], U8, name="xs")
+        xs = keep.tile([P, TOKENS], U8, name="xs")
         nc.gpsimd.memset(xs[:].bitcast(I32), 0)
         offs_sb = load_list(offs, "offs_sb")
         w1_rows = w1.rearrange("(p j) c -> p j c", j=PACK)
-        w1_raw = [keep.tile([P, PACK, HALF], F32, name="w1_raw%d" % h, tag="w_raw%d" % h, align_bytes=64) for h in range(2)]
+        w1_raw = [keep.tile([P, PACK, HALF], F32, name="w1_raw%d" % h, tag="w1_raw%d" % h, align_bytes=64) for h in range(2)]
         nc.sync.dma_start(w1_raw[0][:], w1_rows[:, :, :HALF])
         for q in range(4):
             nc.sync.dma_start(xs[32 * q : 32 * q + 4, :].bitcast(I32), x_scales[0, 4 * q : 4 * q + 4, :].bitcast(I32))
         two_sb = load_list(two, "two_sb")
         nc.sync.dma_start(w1_raw[1][:], w1_rows[:, :, HALF:])
-        xw = keep.tile([P, T], I32, name="xw")
+        xw = keep.tile([P, TOKENS], I32, name="xw")
         nc.sync.dma_start(xw[:], x_words[0].rearrange("p n t -> p (n t)").bitcast(I32))
         ga_sb = keep.tile([P, PACK], F32, name="ga_sb")
         nc.sync.dma_start(ga_sb[:], ga.rearrange("(p t) o -> p (t o)", t=PACK))
@@ -90,13 +96,16 @@ def tile_picked_kqmixhopkindg_none_p_kernel(tc, x_words, x_scales, w1, w2, ga, g
         ident = keep.tile([P, P], F32, name="ident")
         make_identity(nc, ident[:])
 
-        ga_abs = keep.tile([P, PACK], F32, name="ga_abs")
-        nc.scalar.activation(ga_abs[:], ga_sb[:], ABS)
-        sign3 = keep.tile([P, PACK], F32, name="sign3")
-        nc.scalar.activation(sign3[:], ga_sb[:], SIGN)
+        ga_first = keep.tile([P, 1], F32, name="ga_first", tag="ga_first")
+        nc.scalar.activation(ga_first[:], ga_sb[:, :1], ABS)
+        ga_rest = keep.tile([P, PACK - 1], F32, name="ga_rest")
+        nc.scalar.activation(ga_rest[:], ga_sb[:, 1:], ABS)
+        ga_abs = [ga_first[:]] + [ga_rest[:, t : t + 1] for t in range(PACK - 1)]
+        sign_or_zero = keep.tile([P, PACK], F32, name="sign_or_zero")
+        nc.scalar.activation(sign_or_zero[:], ga_sb[:], SIGN)
         sign = keep.tile([P, PACK], F32, name="sign")
-        nc.scalar.activation(sign[:], sign3[:], SIGN, bias=0.5)
-        gb_full = keep.tile([P, PACK], F32, name="gb_full")
+        nc.scalar.activation(sign[:], sign_or_zero[:], SIGN, bias=0.5)
+        gb_full = keep.tile([P, PACK], F32, name="gb_full", tag="gb_full", align_bytes=64)
         for t in range(PACK):
             nc.scalar.activation(gb_full[:, t : t + 1], gb_sb[:, t : t + 1], COPY, scale=sign[:, t : t + 1])
         gb_half = keep.tile([P, PACK], F32, name="gb_half")
@@ -109,70 +118,73 @@ def tile_picked_kqmixhopkindg_none_p_kernel(tc, x_words, x_scales, w1, w2, ga, g
         nc.vector.tensor_copy(xb[1][:], xs[:].indirect(two_sb[:]))
         w1_grouped = keep.tile([P, PACK * N], BF16, name="w1_grouped", align_bytes=64)
         for h in range(2):
-            deal(w1_grouped, w1_raw[h][:], h * P // 2, (h + 1) * P // 2)
+            deal_weights(w1_grouped, w1_raw[h][:], h * P // 2, (h + 1) * P // 2)
         w1q = mx_tiles("w1q", N)
         quantize(w1q, w1_grouped[:])
         xa = [(xa_codes[h], xa_scales[:, h * HALF : (h + 1) * HALF]) for h in range(2)]
         for h in range(2):
-            nc.vector.tensor_copy(xa_codes[h][:], xw[:].bitcast(U32).indirect(offs_sb[:, h * HALF // 16 : (h + 1) * HALF // 16]))
-        last_copy = keep.tile([P, N], F32, name="last_copy", tag="st")
-        a_copy = [win_b[t][:, N:] for t in range(PACK - 1)] + [last_copy[:]]
+            nc.vector.tensor_copy(xa_codes[h][:], xw[:].bitcast(U32).indirect(entries(offs_sb, h)))
+        a_copy_last = keep.tile([P, N], F32, name="a_copy_last", tag="st")
+        a_copy = [win_b[t][:, N:] for t in range(PACK - 1)] + [a_copy_last[:]]
         w2q = mx_tiles("w2q", N)
         for t in range(PACK):
             acc = psum.tile([P, N], F32, name="acc_a", tag="bank_mm")
             for h in range(2):
                 product(acc[:, h * HALF : (h + 1) * HALF], w1q, t, xa[h])
-            nc.scalar.activation(win_a[t][:, :N], acc[:], COPY, scale=ga_abs[:, t : t + 1])
-            if t < 2:
-                nc.scalar.activation(a_copy[t], acc[:], COPY, scale=ga_abs[:, t : t + 1])
+            nc.scalar.activation(win_a[t][:, :N], acc[:], COPY, scale=ga_abs[t])
+            if t < A_BY_SCALAR:
+                nc.scalar.activation(a_copy[t], acc[:], COPY, scale=ga_abs[t])
             else:
                 nc.sync.dma_start(a_copy[t], win_a[t][:, :N])
-        w2_grouped = keep.tile([P, PACK * N], BF16, name="w2_grouped", tag="w2_stage", align_bytes=64)
-        deal(w2_grouped, w2_raw[:], 0, P)
+        w2_grouped = keep.tile([P, PACK * N], BF16, name="w2_grouped", tag="w2_grouped", align_bytes=64)
+        deal_weights(w2_grouped, w2_raw[:], 0, P)
         nc.vector.tensor_copy(xb[0][:], xw[:].bitcast(U32).indirect(two_sb[:]))
 
         sums = [psum.tile([P, PACK, P], F32, name="sums%d" % jb, tag="bank_sum") for jb in range(PACK)]
-        late = keep.tile([P, 6 * N], F32, name="late", tag="w2_raw", align_bytes=64)
-        early = keep.tile([P, 3 * N], F32, name="early", tag="early", align_bytes=64)
-        second = [win_b[PACK - 1][:, N:], early[:, :N], late[:, :N], late[:, N : 2 * N]]
-        rise1 = [early[:, N : 2 * N], early[:, 2 * N :], late[:, 2 * N : 3 * N], late[:, 3 * N : 4 * N]]
-        up1_tiles = [ring.tile([P, N], F32, name="up1") for t in range(PACK)]
-        up3_tiles = [ring.tile([P, N], F32, name="up3") for t in range(PACK)]
-        up1 = [late[:, 4 * N : 5 * N] if t == 1 else up1_tiles[t][:] for t in range(PACK)]
-        up3 = [late[:, 5 * N :] if t == 1 else up3_tiles[t][:] for t in range(PACK)]
-        rise3 = [ring.tile([P, N], F32, name="rise3") for t in range(PACK)]
-        down3 = [ring.tile([P, N], F32, name="down3") for t in range(PACK)]
+        after_w2 = keep.tile([P, 6, N], F32, name="after_w2", tag="w2_raw", align_bytes=64)
+        first_terms = keep.tile([P, 3, N], F32, name="first_terms", tag="first_terms", align_bytes=64)
+        minus_g2 = [win_b[PACK - 1][:, N:], first_terms[:, 0, :], after_w2[:, 0, :], after_w2[:, 1, :]]
+        rise1 = [first_terms[:, 1, :], first_terms[:, 2, :], after_w2[:, 2, :], after_w2[:, 3, :]]
+        up1_own = keep.tile([P, PACK - 1, N], F32, name="up1_own")
+        up1 = [up1_own[:, 0, :], after_w2[:, 4, :], up1_own[:, 1, :], up1_own[:, 2, :]]
+        up3 = after_w2[:, 5, :]
+        rise3 = [keep.tile([P, N], F32, name="rise3_%d" % t, tag="ga_first" if t == 0 else "rise3_%d" % t) for t in range(PACK)]
+        down3 = [keep.tile([P, N], F32, name="down3_%d" % t) for t in range(PACK)]
+        turned = [keep.tile([P, N], BF16, name="turned%d" % jb, tag="turned%d" % jb) for jb in range(PACK)]
 
         def fetch2(t):
-            nc.vector.tensor_scalar(second[t], win_a[t][:].indirect(n2_sb[:]), -1.0, 0.0, ALU.mult, ALU.add)
+            nc.vector.tensor_scalar(minus_g2[t], win_a[t][:].indirect(n2_sb[:]), -1.0, 0.0, ALU.mult, ALU.add)
 
         def fetch1(t):
             nc.vector.tensor_tensor(rise1[t], win_a[t][:].indirect(n1_sb[:]), a_copy[t], ALU.subtract)
             nc.scalar.activation(up1[t], rise1[t], RELU)
 
         def fetch3(t):
-            nc.vector.tensor_tensor(rise3[t][:], win_a[t][:].indirect(n3_sb[:]), second[t], ALU.add)
+            nc.vector.tensor_tensor(rise3[t][:], win_a[t][:].indirect(n3_sb[:]), minus_g2[t], ALU.add)
 
         def clip3(t):
-            if t in ON_VECTOR:
-                nc.vector.tensor_scalar(down3[t][:], rise3[t][:], 0.0, -1.0, ALU.max, ALU.mult)
+            if t == CLIP_ON_SCALAR:
+                nc.scalar.activation(up3, rise3[t][:], RELU)
+                nc.scalar.activation(down3[t][:], up3, COPY, scale=-1.0)
             else:
-                nc.scalar.activation(up3[t], rise3[t][:], RELU)
-                nc.scalar.activation(down3[t][:], up3[t], COPY, scale=-1.0)
+                nc.vector.tensor_scalar(down3[t][:], rise3[t][:], 0.0, -1.0, ALU.max, ALU.mult)
 
         def add_up(t):
-            addends = [win_a[t][:, :N], second[t], down3[t][:], up1[t]]
+            addends = [win_a[t][:, :N], minus_g2[t], down3[t][:], up1[t]]
             for i, addend in enumerate(addends):
                 for jb in range(PACK):
                     nc.tensor.matmul(sums[jb][:, t, :], addend[:, jb * P : (jb + 1) * P], ident[:],
                                      start=(i == 0), stop=(i == len(addends) - 1), is_transpose=True)
 
-        b_full = [keep.tile([P, N], F32, name="b_full%d" % t, tag="b_full%d" % t, align_bytes=64) for t in range(PACK)]
+        def round_pair(jb, e):
+            nc.scalar.copy(out=turned[jb][:, e * HALF : (e + 1) * HALF].rearrange("j (p i) -> j p i", i=2),
+                           in_=sums[jb][:, 2 * e : 2 * e + 2, :].rearrange("j i p -> j p i"))
 
-        def make_b(t):
-            acc = b_acc[t]
-            nc.scalar.activation(win_b[t][:, :N], acc[:], COPY, scale=gb_half[:, t : t + 1])
-            nc.scalar.activation(b_full[t][:], acc[:], COPY, scale=gb_full[:, t : t + 1])
+        b_full = [keep.tile([P, N], F32, name="b_full%d" % t) for t in range(PACK)]
+
+        def copy_b(t):
+            nc.scalar.activation(win_b[t][:, :N], b_acc[t][:], COPY, scale=gb_half[:, t : t + 1])
+            nc.scalar.activation(b_full[t][:], b_acc[t][:], COPY, scale=gb_full[:, t : t + 1])
 
         for t in range(2):
             fetch2(t)
@@ -185,83 +197,64 @@ def tile_picked_kqmixhopkindg_none_p_kernel(tc, x_words, x_scales, w1, w2, ga, g
         for t in range(PACK):
             product(b_acc[t], w2q, t, xb)
         add_up(1)
-        make_b(0)
-        make_b(1)
-        make_b(2)
+        copy_b(0)
         fetch2(2)
         fetch1(2)
+        for jb in range(PACK):
+            round_pair(jb, 0)
+        copy_b(1)
+        copy_b(2)
         fetch3(2)
         fetch2(3)
         clip3(2)
-        make_b(3)
+        copy_b(3)
         add_up(2)
         fetch3(3)
         fetch1(3)
         clip3(3)
         add_up(3)
 
-        tab_tags = ["w_raw0", "w_raw1", "w2_stage", "early"]
+        tab_tags = ["w1_raw0", "w1_raw1", "w2_grouped", "first_terms"]
         win_tab = [keep.tile([P, N], F32, name="win_tab%d" % t, tag=tab_tags[t], align_bytes=64) for t in range(PACK)]
         for t in range(PACK):
             nc.sync.dma_start(win_tab[t][:], tab.rearrange("(p t) c -> p t c", t=PACK)[:, t, :])
 
         st_all = keep.tile([P, PACK * N], F32, name="st_all", tag="st")
         st = [st_all[:, t * N : (t + 1) * N] for t in range(PACK)]
-        win_st = {}
-
-        def entries(lst, h):
-            return lst[:, h * HALF // 16 : (h + 1) * HALF // 16]
-
-        def make_st(t):
+        for t in range(PACK):
             nc.vector.tensor_tensor(st[t], win_b[t][:].indirect(n4_sb[:]), b_full[t][:], ALU.add)
 
-        def copy_st(t):
-            win_st[t] = keep.tile([P, N], F32, name="win_st%d" % t, tag="turn%d" % t if t > 0 else "win_st0")
-            if t < 1:
-                nc.sync.dma_start(win_st[t][:], st[t])
-            else:
-                nc.scalar.copy(win_st[t][:], st[t])
-
-        for t in range(PACK):
-            make_st(t)
-        stage = keep.tile([P, 4 * N], F32, name="stage", tag="b_full2", align_bytes=64)
-        z_stage = stage[:, : 2 * N]
-        z_words = z_stage.rearrange("p (u b m e) -> p b m e u", u=PACK, b=PACK, e=2)
+        z_stage = keep.tile([P, 2 * N], F32, name="z_stage", align_bytes=64)
+        z_words = z_stage[:].rearrange("p (u b m e) -> p u b m e", u=PACK, b=PACK, e=2)
         back = [psum.tile([P, 2, 2, P], F32, name="back", tag="bank_mm") for pair in range(2)]
-
-        def turn_back(jb):
-            pair, b = divmod(jb, 2)
-            turned = keep.tile([P, N], BF16, name="turned%d" % jb, tag="turn%d" % jb)
-            nc.scalar.copy(out=turned[:].rearrange("j (e p i) -> j e p i", e=2, i=2),
-                           in_=sums[jb][:].rearrange("j (e i) p -> j e p i", i=2))
+        for jb in range(PACK):
+            round_pair(jb, 1)
             for e in range(2):
-                nc.tensor.transpose(back[pair][:, b, e, :], turned[:].bitcast(F32)[:, e * P : (e + 1) * P], ident[:])
+                nc.tensor.transpose(back[jb // 2][:, jb % 2, e, :], turned[jb][:].bitcast(F32)[:, e * P : (e + 1) * P], ident[:])
 
-        def deal_z(pair):
-            nc.scalar.copy(out=z_words[:, 2 * pair : 2 * pair + 2], in_=back[pair][:].rearrange("p b e (m u) -> p b m e u", u=PACK))
-
-        for t in range(PACK):
-            turn_back(t)
-            copy_st(t)
-            if t % 2 == 1:
-                deal_z(t // 2)
+        win_st = [keep.tile([P, N], F32, name="win_st%d" % t, tag=("win_st%d" if t < ST_BY_DMA else "turned%d") % t) for t in range(PACK)]
+        for t in range(ST_BY_DMA):
+            nc.sync.dma_start(win_st[t][:], st[t])
+        for pair in range(2):
+            nc.scalar.copy(win_st[ST_BY_DMA + pair][:], st[ST_BY_DMA + pair])
+            nc.scalar.copy(out=z_words[:, :, 2 * pair : 2 * pair + 2], in_=back[pair][:].rearrange("p b e (m u) -> p u b m e", u=PACK))
         zq = mx_tiles("zq", N)
 
-        z2_planes = [stage[:, 2 * N :], stage[:, N : 3 * N]]
+        z2_first = keep.tile([P, 2 * N], F32, name="z2_first", tag="gb_full", align_bytes=64)
+        z2_pairs = [[z2_first[:, :N], z2_first[:, N:]], [z_stage[:, N:], z2_first[:, :N]]]
         z2_grouped = [keep.tile([P, PACK * HALF], BF16, name="z2_grouped%d" % h, align_bytes=64) for h in range(2)]
         z2q = [mx_tiles("z2q%d" % h, HALF) for h in range(2)]
         s_rows = [keep.tile([P, N], F32, name="s_rows%d" % t) for t in range(PACK)]
-        scaled = {}
         s_acc = {}
 
         def hop(h, t):
-            nc.vector.tensor_tensor(z2_planes[h][:, t * HALF : (t + 1) * HALF], win_st[t][:].indirect(entries(n5_sb, h)),
+            nc.vector.tensor_tensor(z2_pairs[h][t // 2][:, t % 2 * HALF : (t % 2 + 1) * HALF], win_st[t][:].indirect(entries(n5_sb, h)),
                                     st[t][:, h * HALF : (h + 1) * HALF], ALU.subtract)
 
-        def group_z2(h):
+        def group_z2(h, planes, t0, t1):
             nc.scalar.copy(
-                out=z2_grouped[h][:].rearrange("p (c i t) -> p c t i", i=4, t=PACK),
-                in_=z2_planes[h].rearrange("p (t c i) -> p c t i", i=4, t=PACK),
+                out=z2_grouped[h][:].rearrange("p (c i t) -> p c t i", i=4, t=PACK)[:, :, t0:t1],
+                in_=planes.rearrange("p (t c i) -> p c t i", i=4, t=t1 - t0),
             )
 
         def make_s(h, t):
@@ -272,37 +265,38 @@ def tile_picked_kqmixhopkindg_none_p_kernel(tc, x_words, x_scales, w1, w2, ga, g
         def halve_s(h, t):
             nc.scalar.activation(win_a[t][:, h * HALF : (h + 1) * HALF], s_acc[h, t][:], COPY, scale=0.03125)
 
+        weighed_own = keep.tile([P, 2 * N], F32, name="weighed_own")
+        weighed = [weighed_own[:, :N], weighed_own[:, N:]] + z2_pairs[1]
+
         def weigh(h, t):
             cols = slice(h * HALF, (h + 1) * HALF)
-            nc.vector.tensor_tensor(scaled[t][:, cols], win_tab[t][:].indirect(entries(n6_sb, h)), s_rows[t][:, cols], ALU.mult)
+            nc.vector.tensor_tensor(weighed[t][:, cols], win_tab[t][:].indirect(entries(n6_sb, h)), s_rows[t][:, cols], ALU.mult)
 
         out_rows = out.rearrange("(p t) v -> p t v", t=PACK)
 
-        def finish(t, pieces):
-            width = N // pieces
-            for i in range(pieces):
+        def finish(t, lists):
+            width = N // len(lists)
+            for i, lst in enumerate(lists):
                 cols = slice(i * width, (i + 1) * width)
                 res = keep.tile([P, width], F32, name="res%d_%d" % (t, i))
-                nc.vector.tensor_tensor(res[:], win_a[t][:].indirect(n7_sb[:, i * width // 16 : (i + 1) * width // 16]), scaled[t][:, cols], ALU.add)
+                nc.vector.tensor_tensor(res[:], win_a[t][:].indirect(lst), weighed[t][:, cols], ALU.add)
                 nc.sync.dma_start(out_rows[:, t, cols], res[:])
 
         for t in range(PACK):
             hop(0, t)
-        quantize(zq, z_stage.bitcast(BF16))
-        group_z2(0)
+        quantize(zq, z_stage[:].bitcast(BF16))
+        group_z2(0, z2_first[:], 0, PACK)
         hop(1, 0)
         hop(1, 1)
         quantize(z2q[0], z2_grouped[0][:])
+        group_z2(1, z2_pairs[1][0], 0, 2)
         hop(1, 2)
         hop(1, 3)
         make_s(0, 0)
         make_s(0, 1)
-        group_z2(1)
+        group_z2(1, z2_pairs[1][1], 2, PACK)
         make_s(0, 2)
         make_s(0, 3)
-        front = keep.tile([P, 2 * N], F32, name="front")
-        scaled[0], scaled[1] = front[:, :N], front[:, N:]
-        scaled[2], scaled[3] = stage[:, N : 2 * N], stage[:, 2 * N : 3 * N]
         weigh(0, 0)
         weigh(0, 1)
         quantize(z2q[1], z2_grouped[1][:])
@@ -315,7 +309,7 @@ def tile_picked_kqmixhopkindg_none_p_kernel(tc, x_words, x_scales, w1, w2, ga, g
             halve_s(0, t)
             halve_s(1, t)
         weigh(1, 0)
-        for t in range(PACK):
-            if t + 1 < PACK:
-                weigh(1, t + 1)
-            finish(t, 2 if t == PACK - 1 else 1)
+        for t in range(PACK - 1):
+            weigh(1, t + 1)
+            finish(t, [n7_sb[:]])
+        finish(PACK - 1, [entries(n7_sb, h) for h in range(2)])

from contextlib import ExitStack

import concourse.mybir as mybir
from concourse.masks import make_identity

K, S, V, H = 512, 512, 512, 512
FLOPS = 2 * K * H * S + 2 * K * H * V + 2 * H * S * V

F32 = mybir.dt.float32
BF16 = mybir.dt.bfloat16
I32 = mybir.dt.int32
U32 = mybir.dt.uint32
U16 = mybir.dt.uint16
U8 = mybir.dt.uint8
FP8X4 = mybir.dt.float8_e4m3fn_x4
ALU = mybir.AluOpType
COPY = mybir.ActivationFunctionType.Copy
RELU = mybir.ActivationFunctionType.Relu
ABS = mybir.ActivationFunctionType.Abs
SIGN = mybir.ActivationFunctionType.Sign

P = 128
PACK = 4
TOKENS = 2048
N = 512
HALF = N // 2
LANES = 16
CLIP_ON_SCALAR = 1
A_BY_SCALAR = 2
ST_BY_DMA = 2


def tile_picked_kqmixhopkindg_none_p_kernel(tc, x_words, x_scales, w1, w2, ga, gb, tab, offs, two, n1, n2, n3, n4, n5, n6, n7, out):
    nc = tc.nc
    with ExitStack() as ctx:
        keep = ctx.enter_context(tc.tile_pool(name="keep", bufs=1))
        psum = ctx.enter_context(tc.psum_pool(name="psum", bufs=PACK))

        def load_list(src, name):
            lst = keep.tile([P, N // LANES], U16, name=name)
            nc.sync.dma_start(lst[:], src)
            return lst

        def entries(lst, h):
            return lst[:, h * HALF // LANES : (h + 1) * HALF // LANES]

        def mx_tiles(name, width):
            codes = keep.tile([P, width], U32, name=name + "_codes", align_bytes=64)
            scales = keep.tile([P, width], U8, name=name + "_scales", align_bytes=64)
            return codes, scales

        def quantize(operand, grouped):
            nc.vector.quantize_mx(out=operand[0][:].bitcast(FP8X4), scales=operand[1][:], in_=grouped)

        def product(acc, lhs, t, rhs):
            cols = slice(t * P, (t + 1) * P)
            nc.tensor.matmul_mx(out=acc[:], lhsT=lhs[0][:, cols].bitcast(FP8X4), lhsT_scale=lhs[1][:, cols],
                                rhs=rhs[0][:].bitcast(FP8X4), rhs_scale=rhs[1][:], start=True, stop=True)

        def deal_weights(grouped, raw, m0, m1):
            nc.scalar.copy(
                out=grouped[:].rearrange("p (u m j) -> p m j u", u=PACK, j=PACK)[:, m0:m1],
                in_=raw.rearrange("p j (m u) -> p m j u", u=PACK),
            )

        xs = keep.tile([P, TOKENS], U8, name="xs")
        nc.gpsimd.memset(xs[:].bitcast(I32), 0)
        offs_sb = load_list(offs, "offs_sb")
        w1_rows = w1.rearrange("(p j) c -> p j c", j=PACK)
        w1_raw = [keep.tile([P, PACK, HALF], F32, name="w1_raw%d" % h, tag="w1_raw%d" % h, align_bytes=64) for h in range(2)]
        nc.sync.dma_start(w1_raw[0][:], w1_rows[:, :, :HALF])
        for q in range(4):
            nc.sync.dma_start(xs[32 * q : 32 * q + 4, :].bitcast(I32), x_scales[0, 4 * q : 4 * q + 4, :].bitcast(I32))
        two_sb = load_list(two, "two_sb")
        nc.sync.dma_start(w1_raw[1][:], w1_rows[:, :, HALF:])
        xw = keep.tile([P, TOKENS], I32, name="xw")
        nc.sync.dma_start(xw[:], x_words[0].rearrange("p n t -> p (n t)").bitcast(I32))
        ga_sb = keep.tile([P, PACK], F32, name="ga_sb")
        nc.sync.dma_start(ga_sb[:], ga.rearrange("(p t) o -> p (t o)", t=PACK))
        n2_sb = load_list(n2, "n2_sb")
        n3_sb = load_list(n3, "n3_sb")
        n1_sb = load_list(n1, "n1_sb")
        gb_sb = keep.tile([P, PACK], F32, name="gb_sb")
        nc.sync.dma_start(gb_sb[:], gb.rearrange("(p t) o -> p (t o)", t=PACK))
        w2_raw = keep.tile([P, PACK, N], F32, name="w2_raw", tag="w2_raw", align_bytes=64)
        nc.sync.dma_start(w2_raw[:], w2.rearrange("(p j) c -> p j c", j=PACK))
        n4_sb = load_list(n4, "n4_sb")
        n5_sb = load_list(n5, "n5_sb")
        n6_sb = load_list(n6, "n6_sb")
        n7_sb = load_list(n7, "n7_sb")

        win_a = [keep.tile([P, 2 * N], F32, name="win_a%d" % t) for t in range(PACK)]
        win_b = [keep.tile([P, 2 * N], F32, name="win_b%d" % t) for t in range(PACK)]
        for win in win_a:
            nc.gpsimd.memset(win[:, N:], 0.0)
        ident = keep.tile([P, P], F32, name="ident")
        make_identity(nc, ident[:])

        ga_first = keep.tile([P, 1], F32, name="ga_first", tag="ga_first")
        nc.scalar.activation(ga_first[:], ga_sb[:, :1], ABS)
        ga_rest = keep.tile([P, PACK - 1], F32, name="ga_rest")
        nc.scalar.activation(ga_rest[:], ga_sb[:, 1:], ABS)
        ga_abs = [ga_first[:]] + [ga_rest[:, t : t + 1] for t in range(PACK - 1)]
        sign_or_zero = keep.tile([P, PACK], F32, name="sign_or_zero")
        nc.scalar.activation(sign_or_zero[:], ga_sb[:], SIGN)
        sign = keep.tile([P, PACK], F32, name="sign")
        nc.scalar.activation(sign[:], sign_or_zero[:], SIGN, bias=0.5)
        gb_full = keep.tile([P, PACK], F32, name="gb_full", tag="gb_full", align_bytes=64)
        for t in range(PACK):
            nc.scalar.activation(gb_full[:, t : t + 1], gb_sb[:, t : t + 1], COPY, scale=sign[:, t : t + 1])
        gb_half = keep.tile([P, PACK], F32, name="gb_half")
        nc.scalar.activation(gb_half[:], gb_full[:], COPY, scale=0.5)

        xa_scales = keep.tile([P, N], U8, name="xa_scales", align_bytes=64)
        xa_codes = [keep.tile([P, HALF], U32, name="xa_codes%d" % h, align_bytes=64) for h in range(2)]
        xb = mx_tiles("xb", N)
        nc.vector.tensor_copy(xa_scales[:], xs[:].indirect(offs_sb[:]))
        nc.vector.tensor_copy(xb[1][:], xs[:].indirect(two_sb[:]))
        w1_grouped = keep.tile([P, PACK * N], BF16, name="w1_grouped", align_bytes=64)
        for h in range(2):
            deal_weights(w1_grouped, w1_raw[h][:], h * P // 2, (h + 1) * P // 2)
        w1q = mx_tiles("w1q", N)
        quantize(w1q, w1_grouped[:])
        xa = [(xa_codes[h], xa_scales[:, h * HALF : (h + 1) * HALF]) for h in range(2)]
        for h in range(2):
            nc.vector.tensor_copy(xa_codes[h][:], xw[:].bitcast(U32).indirect(entries(offs_sb, h)))
        a_copy_last = keep.tile([P, N], F32, name="a_copy_last", tag="st")
        a_copy = [win_b[t][:, N:] for t in range(PACK - 1)] + [a_copy_last[:]]
        w2q = mx_tiles("w2q", N)
        for t in range(PACK):
            acc = psum.tile([P, N], F32, name="acc_a", tag="bank_mm")
            for h in range(2):
                product(acc[:, h * HALF : (h + 1) * HALF], w1q, t, xa[h])
            nc.scalar.activation(win_a[t][:, :N], acc[:], COPY, scale=ga_abs[t])
            if t < A_BY_SCALAR:
                nc.scalar.activation(a_copy[t], acc[:], COPY, scale=ga_abs[t])
            else:
                nc.sync.dma_start(a_copy[t], win_a[t][:, :N])
        w2_grouped = keep.tile([P, PACK * N], BF16, name="w2_grouped", tag="w2_grouped", align_bytes=64)
        deal_weights(w2_grouped, w2_raw[:], 0, P)
        nc.vector.tensor_copy(xb[0][:], xw[:].bitcast(U32).indirect(two_sb[:]))

        sums = [psum.tile([P, PACK, P], F32, name="sums%d" % jb, tag="bank_sum") for jb in range(PACK)]
        after_w2 = keep.tile([P, 6, N], F32, name="after_w2", tag="w2_raw", align_bytes=64)
        first_terms = keep.tile([P, 3, N], F32, name="first_terms", tag="first_terms", align_bytes=64)
        minus_g2 = [win_b[PACK - 1][:, N:], first_terms[:, 0, :], after_w2[:, 0, :], after_w2[:, 1, :]]
        rise1 = [first_terms[:, 1, :], first_terms[:, 2, :], after_w2[:, 2, :], after_w2[:, 3, :]]
        up1_own = keep.tile([P, PACK - 1, N], F32, name="up1_own")
        up1 = [up1_own[:, 0, :], after_w2[:, 4, :], up1_own[:, 1, :], up1_own[:, 2, :]]
        up3 = after_w2[:, 5, :]
        rise3 = [keep.tile([P, N], F32, name="rise3_%d" % t, tag="ga_first" if t == 0 else "rise3_%d" % t) for t in range(PACK)]
        down3 = [keep.tile([P, N], F32, name="down3_%d" % t) for t in range(PACK)]
        turned = [keep.tile([P, N], BF16, name="turned%d" % jb, tag="turned%d" % jb) for jb in range(PACK)]

        def fetch2(t):
            nc.vector.tensor_scalar(minus_g2[t], win_a[t][:].indirect(n2_sb[:]), -1.0, 0.0, ALU.mult, ALU.add)

        def fetch1(t):
            nc.vector.tensor_tensor(rise1[t], win_a[t][:].indirect(n1_sb[:]), a_copy[t], ALU.subtract)
            nc.scalar.activation(up1[t], rise1[t], RELU)

        def fetch3(t):
            nc.vector.tensor_tensor(rise3[t][:], win_a[t][:].indirect(n3_sb[:]), minus_g2[t], ALU.add)

        def clip3(t):
            if t == CLIP_ON_SCALAR:
                nc.scalar.activation(up3, rise3[t][:], RELU)
                nc.scalar.activation(down3[t][:], up3, COPY, scale=-1.0)
            else:
                nc.vector.tensor_scalar(down3[t][:], rise3[t][:], 0.0, -1.0, ALU.max, ALU.mult)

        def add_up(t):
            addends = [win_a[t][:, :N], minus_g2[t], down3[t][:], up1[t]]
            for i, addend in enumerate(addends):
                for jb in range(PACK):
                    nc.tensor.matmul(sums[jb][:, t, :], addend[:, jb * P : (jb + 1) * P], ident[:],
                                     start=(i == 0), stop=(i == len(addends) - 1), is_transpose=True)

        def round_pair(jb, e):
            nc.scalar.copy(out=turned[jb][:, e * HALF : (e + 1) * HALF].rearrange("j (p i) -> j p i", i=2),
                           in_=sums[jb][:, 2 * e : 2 * e + 2, :].rearrange("j i p -> j p i"))

        b_full = [keep.tile([P, N], F32, name="b_full%d" % t) for t in range(PACK)]

        def copy_b(t):
            nc.scalar.activation(win_b[t][:, :N], b_acc[t][:], COPY, scale=gb_half[:, t : t + 1])
            nc.scalar.activation(b_full[t][:], b_acc[t][:], COPY, scale=gb_full[:, t : t + 1])

        for t in range(2):
            fetch2(t)
            fetch1(t)
            fetch3(t)
            clip3(t)
        add_up(0)
        quantize(w2q, w2_grouped[:])
        b_acc = [psum.tile([P, N], F32, name="acc_b", tag="bank_mm") for t in range(PACK)]
        for t in range(PACK):
            product(b_acc[t], w2q, t, xb)
        add_up(1)
        copy_b(0)
        fetch2(2)
        fetch1(2)
        for jb in range(PACK):
            round_pair(jb, 0)
        copy_b(1)
        copy_b(2)
        fetch3(2)
        fetch2(3)
        clip3(2)
        copy_b(3)
        add_up(2)
        fetch3(3)
        fetch1(3)
        clip3(3)
        add_up(3)

        tab_tags = ["w1_raw0", "w1_raw1", "w2_grouped", "first_terms"]
        win_tab = [keep.tile([P, N], F32, name="win_tab%d" % t, tag=tab_tags[t], align_bytes=64) for t in range(PACK)]
        for t in range(PACK):
            nc.sync.dma_start(win_tab[t][:], tab.rearrange("(p t) c -> p t c", t=PACK)[:, t, :])

        st_all = keep.tile([P, PACK * N], F32, name="st_all", tag="st")
        st = [st_all[:, t * N : (t + 1) * N] for t in range(PACK)]
        for t in range(PACK):
            nc.vector.tensor_tensor(st[t], win_b[t][:].indirect(n4_sb[:]), b_full[t][:], ALU.add)

        z_stage = keep.tile([P, 2 * N], F32, name="z_stage", align_bytes=64)
        z_words = z_stage[:].rearrange("p (u b m e) -> p u b m e", u=PACK, b=PACK, e=2)
        back = [psum.tile([P, 2, 2, P], F32, name="back", tag="bank_mm") for pair in range(2)]
        for jb in range(PACK):
            round_pair(jb, 1)
            for e in range(2):
                nc.tensor.transpose(back[jb // 2][:, jb % 2, e, :], turned[jb][:].bitcast(F32)[:, e * P : (e + 1) * P], ident[:])

        win_st = [keep.tile([P, N], F32, name="win_st%d" % t, tag=("win_st%d" if t < ST_BY_DMA else "turned%d") % t) for t in range(PACK)]
        for t in range(ST_BY_DMA):
            nc.sync.dma_start(win_st[t][:], st[t])
        for pair in range(2):
            nc.scalar.copy(win_st[ST_BY_DMA + pair][:], st[ST_BY_DMA + pair])
            nc.scalar.copy(out=z_words[:, :, 2 * pair : 2 * pair + 2], in_=back[pair][:].rearrange("p b e (m u) -> p u b m e", u=PACK))
        zq = mx_tiles("zq", N)

        z2_first = keep.tile([P, 2 * N], F32, name="z2_first", tag="gb_full", align_bytes=64)
        z2_pairs = [[z2_first[:, :N], z2_first[:, N:]], [z_stage[:, N:], z2_first[:, :N]]]
        z2_grouped = [keep.tile([P, PACK * HALF], BF16, name="z2_grouped%d" % h, align_bytes=64) for h in range(2)]
        z2q = [mx_tiles("z2q%d" % h, HALF) for h in range(2)]
        s_rows = [keep.tile([P, N], F32, name="s_rows%d" % t) for t in range(PACK)]
        s_acc = {}

        def hop(h, t):
            nc.vector.tensor_tensor(z2_pairs[h][t // 2][:, t % 2 * HALF : (t % 2 + 1) * HALF], win_st[t][:].indirect(entries(n5_sb, h)),
                                    st[t][:, h * HALF : (h + 1) * HALF], ALU.subtract)

        def group_z2(h, planes, t0, t1):
            nc.scalar.copy(
                out=z2_grouped[h][:].rearrange("p (c i t) -> p c t i", i=4, t=PACK)[:, :, t0:t1],
                in_=planes.rearrange("p (t c i) -> p c t i", i=4, t=t1 - t0),
            )

        def make_s(h, t):
            s_acc[h, t] = psum.tile([P, HALF], F32, name="acc_s", tag=("bank_mm", "bank_sum")[h])
            product(s_acc[h, t], zq, t, z2q[h])
            nc.scalar.activation(s_rows[t][:, h * HALF : (h + 1) * HALF], s_acc[h, t][:], COPY, scale=-0.0625)

        def halve_s(h, t):
            nc.scalar.activation(win_a[t][:, h * HALF : (h + 1) * HALF], s_acc[h, t][:], COPY, scale=0.03125)

        weighed_own = keep.tile([P, 2 * N], F32, name="weighed_own")
        weighed = [weighed_own[:, :N], weighed_own[:, N:]] + z2_pairs[1]

        def weigh(h, t):
            cols = slice(h * HALF, (h + 1) * HALF)
            nc.vector.tensor_tensor(weighed[t][:, cols], win_tab[t][:].indirect(entries(n6_sb, h)), s_rows[t][:, cols], ALU.mult)

        out_rows = out.rearrange("(p t) v -> p t v", t=PACK)

        def finish(t, lists):
            width = N // len(lists)
            for i, lst in enumerate(lists):
                cols = slice(i * width, (i + 1) * width)
                res = keep.tile([P, width], F32, name="res%d_%d" % (t, i))
                nc.vector.tensor_tensor(res[:], win_a[t][:].indirect(lst), weighed[t][:, cols], ALU.add)
                nc.sync.dma_start(out_rows[:, t, cols], res[:])

        for t in range(PACK):
            hop(0, t)
        quantize(zq, z_stage[:].bitcast(BF16))
        group_z2(0, z2_first[:], 0, PACK)
        hop(1, 0)
        hop(1, 1)
        quantize(z2q[0], z2_grouped[0][:])
        group_z2(1, z2_pairs[1][0], 0, 2)
        hop(1, 2)
        hop(1, 3)
        make_s(0, 0)
        make_s(0, 1)
        group_z2(1, z2_pairs[1][1], 2, PACK)
        make_s(0, 2)
        make_s(0, 3)
        weigh(0, 0)
        weigh(0, 1)
        quantize(z2q[1], z2_grouped[1][:])
        weigh(0, 2)
        weigh(0, 3)
        make_s(1, 0)
        for t in range(PACK):
            if t + 1 < PACK:
                make_s(1, t + 1)
            halve_s(0, t)
            halve_s(1, t)
        weigh(1, 0)
        for t in range(PACK - 1):
            weigh(1, t + 1)
            finish(t, [n7_sb[:]])
        finish(PACK - 1, [entries(n7_sb, h) for h in range(2)])
